import numpy as np
import ml_dtypes


def mxq(x, axis, fmt="e4m3"):
    dtype, down = {"e4m3": (ml_dtypes.float8_e4m3fn, 7), "e5m2": (ml_dtypes.float8_e5m2, 14)}[fmt]
    v = np.moveaxis(np.asarray(x, np.float32).astype(ml_dtypes.bfloat16).astype(np.float64), axis, -1)
    blocks = v.reshape(v.shape[:-1] + (-1, 32))
    amax = np.abs(blocks).max(-1, keepdims=True)
    byte = np.maximum(np.where(amax > 0, np.frexp(amax)[1] - 1 + 127, 0) - down, 1)
    scale = np.exp2(byte - 127.0)
    codes = (blocks / scale).astype(np.float32).astype(dtype).astype(np.float64)
    return np.moveaxis((codes * scale).reshape(v.shape), -1, axis)


WIDE = False


def mx_kscale(k):
    if not WIDE:
        return np.ones(k)
    levels = np.array([10, -10, 5, -5, 0])
    if k % 512:
        return np.exp2(np.random.permutation(np.resize(levels, k // 32))).repeat(32)
    a = np.empty((k // 512, 16))
    for p in range(k // 512):
        a[p, :8] = np.random.permutation(np.resize(levels, 8))
        for g in range(8):
            far = levels[np.abs(levels - a[p, g]) >= 10]
            a[p, g + 8] = far[np.random.randint(len(far))]
    return np.exp2(a.ravel()).repeat(32)


BF16 = ml_dtypes.bfloat16


def bf(x):
    return np.asarray(x, np.float32).astype(BF16)


def f64(x):
    return np.asarray(x).astype(np.float64)


M, N, KX, KY, D = 1536, 512, 1024, 1536, 1024

RATE = 2.0


def sigmoid(v):
    return 1.0 / (1.0 + np.exp(-v))


def draw0():
    s, r, t = mx_kscale(KX), mx_kscale(KY), mx_kscale(D)
    return {"x": bf(np.random.standard_normal((M, KX)) * s),
            "wx": bf(1.5 * np.random.standard_normal((KX, D)) / np.sqrt(KX) / s[:, None]),
            "bx": bf(0.4 * np.random.standard_normal(D)),
            "lx": bf(np.exp(0.3 * np.random.standard_normal(D)) * t),
            "y": bf(np.random.standard_normal((N, KY)) * r),
            "wy": bf(1.5 * np.random.standard_normal((KY, D)) / np.sqrt(KY) / r[:, None]),
            "by": bf(0.4 * np.random.standard_normal(D)),
            "wg": bf(np.random.standard_normal((KY, D)) / np.sqrt(KY) / r[:, None]),
            "bg": bf(0.5 * np.random.standard_normal(D)),
            "ly": bf(np.exp(0.3 * np.random.standard_normal(D)) / t),
            "ex": bf(0.5 * np.abs(np.random.standard_normal(M))),
            "ey": bf(0.5 * np.abs(np.random.standard_normal(N)))}


def core(x, wx, bx, lx, y, wy, by, wg, bg, ly, ex, ey):
    zx = mxq(f64(x), 1, "e4m3") @ mxq(f64(wx), 0, "e4m3")
    a = np.tanh(zx + f64(bx)) * f64(lx)
    yq = mxq(f64(y), 1, "e4m3")
    zy = yq @ mxq(f64(wy), 0, "e4m3")
    zg = yq @ mxq(f64(wg), 0, "e4m3")
    b = sigmoid(zg + f64(bg)) * np.tanh(zy + f64(by)) * f64(ly)
    c = mxq(a, 1, "e4m3") @ mxq(b, 1, "e4m3").T
    return np.exp(RATE / np.sqrt(D) * c - f64(ex)[:, None] - f64(ey)[None, :])


def e4m3fn_bytes(y):
    return np.clip(np.asarray(y, np.float64), -448.0, 448.0).astype(np.float32).astype(ml_dtypes.float8_e4m3fn).view(np.uint8)


def e4m3fn_values(b):
    return np.asarray(b, np.uint8).view(ml_dtypes.float8_e4m3fn).astype(np.float64)


def setup_inputs():
    d = draw0()
    x0 = np.asarray(d['x']).astype(np.float64)
    s = (np.max(np.abs(x0), axis=(0,), keepdims=True) / 448.0).astype(np.float32)
    out = {}
    for k, v in d.items():
        if k == 'x':
            out['x_bytes'] = e4m3fn_bytes(x0 / s.astype(np.float64))
            out['x_scale'] = s
        else:
            out[k] = v
    return out


def reference(x_bytes, x_scale, wx, bx, lx, y, wy, by, wg, bg, ly, ex, ey):
    return core(e4m3fn_values(x_bytes) * x_scale.astype(np.float64), wx, bx, lx, y, wy, by, wg, bg, ly, ex, ey)

@@ -1,0 +1,487 @@
+from contextlib import ExitStack
+
+import concourse.mybir as mybir
+from concourse.masks import make_identity
+
+M, N, KX, KY, D = 1536, 512, 1024, 1536, 1024
+RATE = 2.0
+FLOPS = 2 * M * KX * D + 2 * 2 * N * KY * D + 2 * M * N * D
+
+F32 = mybir.dt.float32
+BF16 = mybir.dt.bfloat16
+U32 = mybir.dt.uint32
+U8 = mybir.dt.uint8
+FP8 = mybir.dt.float8_e4m3fn
+FP8X4 = mybir.dt.float8_e4m3fn_x4
+ACT = mybir.ActivationFunctionType
+ALU = mybir.AluOpType
+ENG = mybir.EngineType
+
+P = 128
+PACK = 4
+KP = P * PACK
+GROUPS = D // KP
+TOK = 512
+NT = M // TOK
+QT = TOK // P
+XP = KX // KP
+YP = KY // KP
+
+
+def tile_split_tree_kinship_f5_kernel(tc, x_bytes, x_scale, wx, bx, lx, y, wy, by, wg, bg, ly, ex, ey, out):
+    nc = tc.nc
+    with ExitStack() as ctx:
+        keep = ctx.enter_context(tc.tile_pool(name="keep", bufs=1))
+        rawp = ctx.enter_context(tc.tile_pool(name="rawp", bufs=6))
+        inx = ctx.enter_context(tc.tile_pool(name="inx", bufs=2))
+        iny = ctx.enter_context(tc.tile_pool(name="iny", bufs=2))
+        xsp = ctx.enter_context(tc.tile_pool(name="xsp", bufs=3))
+        tnh = ctx.enter_context(tc.tile_pool(name="tnh", bufs=4))
+        grp = ctx.enter_context(tc.tile_pool(name="grp", bufs=8))
+        fin = ctx.enter_context(tc.tile_pool(name="fin", bufs=5))
+        ps1 = ctx.enter_context(tc.psum_pool(name="ps1", bufs=5))
+        ps2 = ctx.enter_context(tc.psum_pool(name="ps2", bufs=3))
+
+        ident = keep.tile([P, P], F32, name="ident")
+        make_identity(nc, ident[:])
+        scale_b = keep.tile([P, KX], F32, name="scale_b", align_bytes=64)
+        warm = keep.tile([P, 1], F32, name="warm")
+        nc.vector.memset(warm[:], 0.0)
+        nc.scalar.activation(out=warm[:], in_=warm[:], func=ACT.Tanh)
+
+        raws, x8, yraw, vecs = {}, {}, {}, {}
+        wsrc = {"x": wx, "y": wy, "g": wg}
+
+        def load_w(nm, k, c0=0, c1=D):
+            if c0 == 0:
+                raws[nm, k] = rawp.tile([P, PACK, D], BF16, name="raw")
+            src = wsrc[nm].rearrange("(k p j) c -> k p j c", p=P, j=PACK)[k]
+            nc.sync.dma_start(out=raws[nm, k][:, :, c0:c1], in_=src[:, :, c0:c1])
+
+        xv = x_bytes.rearrange("(p q) k -> p q k", q=M // P)
+        yv = y.rearrange("(q p) (k w) -> k p q w", p=P, w=KP)
+
+        def load_x(i):
+            x8[i] = inx.tile([P, QT, KX], U8, name="x8")
+            nc.sync.dma_start(out=x8[i][:], in_=xv[:, QT * i : QT * (i + 1), :])
+
+        def load_y(k):
+            yraw[k] = iny.tile([P, QT, KP], BF16, name="yraw")
+            nc.sync.dma_start(out=yraw[k][:], in_=yv[k])
+
+        def load_scale():
+            nc.sync.dma_start(out=scale_b[:], in_=x_scale.rearrange("o k -> (o k)").partition_broadcast(P))
+
+        def load_vecs():
+            for nm, v in (("bx", bx), ("lx", lx), ("by", by), ("bg", bg), ("ly", ly)):
+                vecs[nm] = keep.tile([P, GROUPS, PACK], BF16, name="v_" + nm)
+                nc.sync.dma_start(out=vecs[nm][:], in_=v.rearrange("(g p t) -> p g t", p=P, t=PACK))
+
+        exb = keep.tile([P, M // P], BF16, name="exb")
+        eyb = keep.tile([P, N], BF16, name="eyb")
+
+        def load_e():
+            nc.sync.dma_start(out=exb[:], in_=ex.rearrange("(p q) -> p q", q=M // P))
+            nc.sync.dma_start(out=eyb[:], in_=ey.partition_broadcast(P))
+
+        load_w("x", 0, 0, KP)
+        load_w("x", 1, 0, KP)
+        load_scale()
+        load_x(0)
+        load_w("x", 0, KP, D)
+        load_w("x", 1, KP, D)
+        load_w("y", 0)
+        load_w("g", 0)
+        load_vecs()
+        load_x(1)
+        load_w("y", 1)
+        load_w("g", 1)
+        for k in range(YP):
+            load_y(k)
+        load_w("y", 2)
+        load_w("g", 2)
+        load_x(2)
+        load_e()
+
+        bxf = keep.tile([P, GROUPS, PACK], F32, name="bxf")
+        byf = keep.tile([P, GROUPS, PACK], F32, name="byf")
+        bgh = keep.tile([P, GROUPS, PACK], F32, name="bgh")
+        lyh = keep.tile([P, GROUPS, PACK], F32, name="lyh")
+        lxf = keep.tile([P, GROUPS, PACK], F32, name="lxf")
+        nex = keep.tile([P, M // P], F32, name="nex")
+        nc.gpsimd.tensor_copy(out=bxf[:], in_=vecs["bx"][:])
+        nc.gpsimd.tensor_copy(out=byf[:], in_=vecs["by"][:])
+        nc.gpsimd.tensor_copy(out=lxf[:], in_=vecs["lx"][:])
+        nc.gpsimd.tensor_scalar(out=bgh[:], in0=vecs["bg"][:], scalar1=0.5, scalar2=None, op0=ALU.mult)
+        nc.gpsimd.tensor_scalar(out=lyh[:], in0=vecs["ly"][:], scalar1=0.5, scalar2=None, op0=ALU.mult)
+        nc.gpsimd.tensor_scalar(out=nex[:], in0=exb[:], scalar1=-1.0, scalar2=None, op0=ALU.mult)
+
+        def copy(eng, out, in_):
+            if eng == "s":
+                nc.scalar.copy(out=out, in_=in_)
+            else:
+                nc.vector.tensor_copy(out=out, in_=in_)
+
+        def quant(key, src):
+            code = keep.tile([P, KP], U32, name="code_" + key, align_bytes=64)
+            sc = keep.tile([P, KP], U8, name="scal_" + key, align_bytes=64)
+            nc.vector.quantize_mx(out=code[:].bitcast(FP8X4), scales=sc[:], in_=src)
+            return code, sc
+
+        def new_group():
+            return grp.tile([P, PACK * KP], BF16, name="grouped", align_bytes=64)
+
+        wc, wg_t, wps = {}, {}, {}
+
+        def w_src(nm, k, c):
+            return raws[nm, k][:, :, KP * c : KP * (c + 1)]
+
+        def il(nm, k, c, eng):
+            g = wg_t[nm, k, c] = new_group()
+            copy(eng, g[:].rearrange("p (t m j) -> p m j t", t=PACK, j=PACK),
+                 w_src(nm, k, c).rearrange("p j (m t) -> p m j t", t=PACK))
+
+        def qw(nm, k, c):
+            wc[nm, k, c] = quant("w%s%d%d" % (nm, k, c), wg_t[nm, k, c][:])
+
+        xst, xb, xg, xc_ = {}, {}, {}, {}
+
+        def xs(q):
+            xst[q] = xsp.tile([P, KX], BF16, name="xs", align_bytes=64)
+            nc.vector.tensor_tensor(out=xst[q][:], in0=x8[q // QT][:, q % QT, :].bitcast(FP8), in1=scale_b[:], op=ALU.mult)
+
+        def xt(q):
+            xb[q] = ps2.tile([P, XP, 2, P], F32, name="tr")
+            words = xst[q][:].bitcast(F32)
+            for k in range(XP):
+                for u in range(2):
+                    nc.tensor.transpose(xb[q][:, k, u, :], words[:, 256 * k + u : 256 * (k + 1) : 2], ident[:])
+
+        def xc(q, eng="s"):
+            i, r = divmod(q, QT)
+            if r == 0:
+                for k in range(XP):
+                    xg[i, k] = new_group()
+            for k in range(XP):
+                copy(eng, xg[i, k][:, KP * r : KP * (r + 1)].bitcast(F32).rearrange("p (r u) -> p r u", u=2),
+                     xb[q][:, k, :, :].rearrange("p u r -> p r u"))
+
+        def xq(i, k):
+            xc_[i, k] = quant("x%d%d" % (i, k), xg[i, k][:])
+
+        yb, yg, yc_ = {}, {}, {}
+
+        def yt(k, h):
+            yb[k, h] = ps2.tile([P, 2, 2, P], F32, name="tr")
+            for q in range(2):
+                words = yraw[k][:, 2 * h + q, :].bitcast(F32)
+                for u in range(2):
+                    nc.tensor.transpose(yb[k, h][:, q, u, :], words[:, u::2], ident[:])
+
+        def yc(k, h, eng="s"):
+            if h == 0:
+                yg[k] = new_group()
+            copy(eng, yg[k][:, 2 * N * h : 2 * N * (h + 1)].bitcast(F32).rearrange("p (q r u) -> p q r u", q=2, u=2),
+                 yb[k, h][:].rearrange("p q u r -> p q r u"))
+
+        def yq(k):
+            yc_[k] = quant("y%d" % k, yg[k][:])
+
+        def mx(bank, lhs, cols, rhs):
+            for k in range(len(lhs)):
+                (lc, ls), (rc, rs) = lhs[k], rhs[k]
+                nc.tensor.matmul_mx(out=bank, lhsT=lc[:, cols].bitcast(FP8X4), lhsT_scale=ls[:, cols],
+                                    rhs=rc[:].bitcast(FP8X4), rhs_scale=rs[:], start=(k == 0), stop=(k == len(lhs) - 1))
+
+        def stepped(tile):
+            return tile[:].rearrange("p t (c i) -> p c t i", i=4)
+
+        def woven(tile):
+            return tile[:].rearrange("p (c i t) -> p c t i", i=4, t=PACK)
+
+        pb, tb_, pa, ta_, gb, ga, bc_, ac_, pc, dd = {}, {}, {}, {}, {}, {}, {}, {}, {}, {}
+
+        def mb(c, t, nm):
+            pb[c, t, nm] = ps1.tile([P, N], F32, name="s1")
+            mx(pb[c, t, nm][:], [wc[nm, k, c] for k in range(YP)], slice(P * t, P * (t + 1)), [yc_[k] for k in range(YP)])
+
+        def tb(c, t, nm):
+            if (c, nm) not in tb_:
+                tb_[c, nm] = tnh.tile([P, PACK, N], F32, name="tanh")
+            b, s = (bgh, 0.5) if nm == "g" else (byf, 1.0)
+            nc.scalar.activation(out=tb_[c, nm][:, t, :], in_=pb[c, t, nm][:], func=ACT.Tanh, bias=b[:, c, t : t + 1], scale=s)
+
+        def bts(c, t):
+            g = tb_[c, "g"][:, t, :]
+            l = lyh[:, c, t : t + 1]
+            nc.vector.tensor_scalar(out=g, in0=g, scalar1=l, scalar2=l, op0=ALU.mult, op1=ALU.add)
+
+        def bm(c):
+            gb[c] = new_group()
+            nc.vector.tensor_tensor(out=woven(gb[c]), in0=stepped(tb_[c, "g"]), in1=stepped(tb_[c, "y"]), op=ALU.mult)
+
+        def bq(c):
+            bc_[c] = quant("b%d" % c, gb[c][:])
+
+        def ma(i, c, t):
+            pa[i, c, t] = ps1.tile([P, TOK], F32, name="s1")
+            mx(pa[i, c, t][:], [wc["x", k, c] for k in range(XP)], slice(P * t, P * (t + 1)), [xc_[i, k] for k in range(XP)])
+
+        def ta(i, c, t):
+            if (i, c) not in ta_:
+                ta_[i, c] = tnh.tile([P, PACK, TOK], F32, name="tanh")
+            nc.scalar.activation(out=ta_[i, c][:, t, :], in_=pa[i, c, t][:], func=ACT.Tanh, bias=bxf[:, c, t : t + 1], scale=1.0)
+
+        def am(i, c):
+            ga[i, c] = new_group()
+            l = lxf[:, c, :].unsqueeze(1).unsqueeze(3).to_broadcast([P, TOK // 4, PACK, 4])
+            nc.vector.tensor_tensor(out=woven(ga[i, c]), in0=stepped(ta_[i, c]), in1=l, op=ALU.mult)
+
+        def aq(i, c):
+            ac_[i, c] = quant("a%d%d" % (i, c), ga[i, c][:])
+
+        ov = out.rearrange("(p q) j -> p q j", q=M // P)
+
+        def mc(q):
+            i, r = divmod(q, QT)
+            pc[q] = ps2.tile([P, N], F32, name="tr")
+            mx(pc[q][:], [ac_[i, c] for c in range(GROUPS)], slice(P * r, P * (r + 1)), [bc_[c] for c in range(GROUPS)])
+
+        def st(q):
+            dd[q] = fin.tile([P, N], F32, name="d")
+            nc.vector.scalar_tensor_tensor(out=dd[q][:], in0=pc[q][:], scalar=RATE / D**0.5, in1=eyb[:], op0=ALU.mult, op1=ALU.subtract)
+
+        def ex_(q):
+            nc.scalar.activation(out=dd[q][:], in_=dd[q][:], func=ACT.Exp, bias=nex[:, q : q + 1], scale=1.0)
+            nc.sync.dma_start(out=ov[:, q, :], in_=dd[q][:])
+
+        ctx.enter_context(tc.manual_schedule(engines={ENG.DVE, ENG.Activation, ENG.PE}))
+        il("x", 0, 0, "s")
+        il("x", 1, 0, "v")
+        qw("x", 0, 0)
+        qw("x", 1, 0)
+        xs(0)
+        xs(1)
+        il("x", 0, 1, "s")
+        xt(0)
+        xs(2)
+        xt(1)
+        xs(3)
+        xt(2)
+        xc(0)
+        xc(1)
+        il("y", 0, 0, "v")
+        xt(3)
+        xc(2)
+        xc(3)
+        qw("x", 0, 1)
+        il("y", 0, 1, "s")
+        xq(0, 0)
+        xq(0, 1)
+        qw("y", 0, 0)
+        ma(0, 0, 0)
+        il("g", 0, 1, "v")
+        ma(0, 0, 1)
+        ta(0, 0, 0)
+        ma(0, 0, 2)
+        ta(0, 0, 1)
+        ma(0, 0, 3)
+        xs(4)
+        ta(0, 0, 2)
+        ta(0, 0, 3)
+        xs(5)
+        xt(4)
+        il("g", 0, 0, "s")
+        am(0, 0)
+        xt(5)
+        xc(4)
+        xs(6)
+        xc(5)
+        yt(0, 0)
+        il("y", 1, 0, "s")
+        yt(0, 1)
+        aq(0, 0)
+        xt(6)
+        xs(7)
+        qw("g", 0, 0)
+        xc(6)
+        qw("y", 1, 0)
+        yc(0, 0)
+        xt(7)
+        il("g", 1, 0, "v")
+        yc(0, 1)
+        yt(1, 0)
+        xc(7)
+        yt(1, 1)
+        yq(0)
+        yc(1, 0)
+        yt(2, 0)
+        xq(1, 0)
+        yc(1, 1)
+        yt(2, 1)
+        xq(1, 1)
+        yc(2, 0)
+        il("y", 2, 0, "v")
+        ma(1, 0, 0)
+        yc(2, 1)
+        ma(1, 0, 1)
+        ta(1, 0, 0)
+        ma(1, 0, 2)
+        yq(1)
+        ta(1, 0, 1)
+        ma(1, 0, 3)
+        il("g", 2, 1, "v")
+        ta(1, 0, 2)
+        ta(1, 0, 3)
+        qw("y", 2, 0)
+        il("y", 2, 1, "s")
+        qw("g", 2, 1)
+        xs(8)
+        xs(9)
+        xt(8)
+        il("y", 1, 1, "s")
+        xs(10)
+        xt(9)
+        xs(11)
+        xt(10)
+        xc(8)
+        xc(9)
+        yq(2)
+        xt(11)
+        xc(10)
+        qw("y", 2, 1)
+        mb(0, 0, "y")
+        il("g", 2, 0, "v")
+        xc(11)
+        mb(0, 1, "y")
+        tb(0, 0, "y")
+        mb(0, 2, "y")
+        xq(2, 0)
+        tb(0, 1, "y")
+        xq(2, 1)
+        il("g", 1, 1, "s")
+        mb(0, 3, "y")
+        qw("g", 2, 0)
+        ma(2, 0, 0)
+        am(1, 0)
+        ma(2, 0, 1)
+        ma(2, 0, 2)
+        tb(0, 2, "y")
+        tb(0, 3, "y")
+        ma(2, 0, 3)
+        qw("y", 1, 1)
+        ta(2, 0, 0)
+        aq(1, 0)
+        ta(2, 0, 1)
+        qw("g", 1, 0)
+        ta(2, 0, 2)
+        qw("y", 0, 1)
+        mb(0, 0, "g")
+        ta(2, 0, 3)
+        qw("g", 1, 1)
+        il("x", 1, 1, "s")
+        mb(0, 1, "g")
+        am(2, 0)
+        mb(0, 2, "g")
+        mb(0, 3, "g")
+        tb(0, 0, "g")
+        qw("g", 0, 1)
+        mb(1, 0, "y")
+        tb(0, 1, "g")
+        bts(0, 0)
+        mb(1, 0, "g")
+        aq(2, 0)
+        tb(0, 2, "g")
+        bts(0, 1)
+        tb(0, 3, "g")
+        mb(1, 1, "g")
+        bts(0, 2)
+        qw("x", 1, 1)
+        tb(1, 0, "g")
+        mb(1, 2, "g")
+        bts(0, 3)
+        tb(1, 1, "g")
+        bts(1, 0)
+        bm(0)
+        ma(1, 1, 0)
+        tb(1, 2, "g")
+        ma(1, 1, 1)
+        ta(1, 1, 0)
+        ma(1, 1, 2)
+        ta(1, 1, 1)
+        ma(1, 1, 3)
+        ta(1, 1, 2)
+        bts(1, 1)
+        mb(1, 3, "g")
+        bq(0)
+        ta(1, 1, 3)
+        bts(1, 2)
+        tb(1, 0, "y")
+        mb(1, 1, "y")
+        am(1, 1)
+        tb(1, 3, "g")
+        mb(1, 2, "y")
+        tb(1, 1, "y")
+        mb(1, 3, "y")
+        tb(1, 2, "y")
+        bts(1, 3)
+        ma(0, 1, 0)
+        tb(1, 3, "y")
+        aq(1, 1)
+        ma(0, 1, 1)
+        ta(0, 1, 0)
+        bm(1)
+        ma(0, 1, 2)
+        ta(0, 1, 1)
+        ma(0, 1, 3)
+        ta(0, 1, 2)
+        ma(2, 1, 0)
+        ta(0, 1, 3)
+        ma(2, 1, 1)
+        ta(2, 1, 0)
+        am(0, 1)
+        ma(2, 1, 2)
+        ta(2, 1, 1)
+        ma(2, 1, 3)
+        ta(2, 1, 2)
+        ta(2, 1, 3)
+        bq(1)
+        aq(0, 1)
+        mc(4)
+        am(2, 1)
+        mc(0)
+        mc(1)
+        st(0)
+        st(1)
+        mc(2)
+        ex_(0)
+        aq(2, 1)
+        mc(3)
+        ex_(1)
+        st(2)
+        st(3)
+        mc(8)
+        ex_(2)
+        st(4)
+        mc(9)
+        ex_(3)
+        st(8)
+        mc(10)
+        ex_(4)
+        st(9)
+        mc(11)
+        ex_(8)
+        st(10)
+        mc(5)
+        ex_(9)
+        st(11)
+        mc(6)
+        ex_(10)
+        st(5)
+        mc(7)
+        ex_(11)
+        st(6)
+        ex_(5)
+        st(7)
+        ex_(6)
+        ex_(7)

@@ -38,7 +38,7 @@ def tile_split_tree_kinship_f5_kernel(tc, x_bytes, x_scale, wx, bx, lx, y, wy, b
         xsp = ctx.enter_context(tc.tile_pool(name="xsp", bufs=3))
         tnh = ctx.enter_context(tc.tile_pool(name="tnh", bufs=4))
         grp = ctx.enter_context(tc.tile_pool(name="grp", bufs=8))
-        fin = ctx.enter_context(tc.tile_pool(name="fin", bufs=5))
+        fin = ctx.enter_context(tc.tile_pool(name="fin", bufs=4))
         ps1 = ctx.enter_context(tc.psum_pool(name="ps1", bufs=5))
         ps2 = ctx.enter_context(tc.psum_pool(name="ps2", bufs=3))
 
@@ -52,22 +52,21 @@ def tile_split_tree_kinship_f5_kernel(tc, x_bytes, x_scale, wx, bx, lx, y, wy, b
         raws, x8, yraw, vecs = {}, {}, {}, {}
         wsrc = {"x": wx, "y": wy, "g": wg}
 
-        def load_w(nm, k, c0=0, c1=D):
-            if c0 == 0:
-                raws[nm, k] = rawp.tile([P, PACK, D], BF16, name="raw")
-            src = wsrc[nm].rearrange("(k p j) c -> k p j c", p=P, j=PACK)[k]
-            nc.sync.dma_start(out=raws[nm, k][:, :, c0:c1], in_=src[:, :, c0:c1])
+        def load_w(nm, k):
+            raws[nm, k] = rawp.tile([P, PACK, D], BF16, name="raw")
+            nc.sync.dma_start(out=raws[nm, k][:], in_=wsrc[nm].rearrange("(k p j) c -> k p j c", p=P, j=PACK)[k])
 
         xv = x_bytes.rearrange("(p q) k -> p q k", q=M // P)
-        yv = y.rearrange("(q p) (k w) -> k p q w", p=P, w=KP)
+        yv = y.rearrange("(h q p) k -> h p q k", q=2, p=P)
 
-        def load_x(i):
-            x8[i] = inx.tile([P, QT, KX], U8, name="x8")
-            nc.sync.dma_start(out=x8[i][:], in_=xv[:, QT * i : QT * (i + 1), :])
+        def load_x(i, lo=0, hi=QT):
+            if lo == 0:
+                x8[i] = inx.tile([P, QT, KX], U8, name="x8")
+            nc.sync.dma_start(out=x8[i][:, lo:hi, :], in_=xv[:, QT * i + lo : QT * i + hi, :])
 
-        def load_y(k):
-            yraw[k] = iny.tile([P, QT, KP], BF16, name="yraw")
-            nc.sync.dma_start(out=yraw[k][:], in_=yv[k])
+        def load_y(h):
+            yraw[h] = iny.tile([P, 2, KY], BF16, name="yraw")
+            nc.sync.dma_start(out=yraw[h][:], in_=yv[h])
 
         def load_scale():
             nc.sync.dma_start(out=scale_b[:], in_=x_scale.rearrange("o k -> (o k)").partition_broadcast(P))
@@ -84,23 +83,21 @@ def tile_split_tree_kinship_f5_kernel(tc, x_bytes, x_scale, wx, bx, lx, y, wy, b
             nc.sync.dma_start(out=exb[:], in_=ex.rearrange("(p q) -> p q", q=M // P))
             nc.sync.dma_start(out=eyb[:], in_=ey.partition_broadcast(P))
 
-        load_w("x", 0, 0, KP)
-        load_w("x", 1, 0, KP)
+        load_w("x", 0)
         load_scale()
         load_x(0)
-        load_w("x", 0, KP, D)
-        load_w("x", 1, KP, D)
+        load_w("x", 1)
         load_w("y", 0)
         load_w("g", 0)
-        load_vecs()
         load_x(1)
         load_w("y", 1)
         load_w("g", 1)
-        for k in range(YP):
-            load_y(k)
+        load_y(0)
+        load_y(1)
         load_w("y", 2)
         load_w("g", 2)
         load_x(2)
+        load_vecs()
         load_e()
 
         bxf = keep.tile([P, GROUPS, PACK], F32, name="bxf")
@@ -131,7 +128,7 @@ def tile_split_tree_kinship_f5_kernel(tc, x_bytes, x_scale, wx, bx, lx, y, wy, b
         def new_group():
             return grp.tile([P, PACK * KP], BF16, name="grouped", align_bytes=64)
 
-        wc, wg_t, wps = {}, {}, {}
+        wc, wg_t = {}, {}
 
         def w_src(nm, k, c):
             return raws[nm, k][:, :, KP * c : KP * (c + 1)]
@@ -159,7 +156,7 @@ def tile_split_tree_kinship_f5_kernel(tc, x_bytes, x_scale, wx, bx, lx, y, wy, b
 
         def xc(q, eng="s"):
             i, r = divmod(q, QT)
-            if r == 0:
+            if (i, 0) not in xg:
                 for k in range(XP):
                     xg[i, k] = new_group()
             for k in range(XP):
@@ -174,12 +171,12 @@ def tile_split_tree_kinship_f5_kernel(tc, x_bytes, x_scale, wx, bx, lx, y, wy, b
         def yt(k, h):
             yb[k, h] = ps2.tile([P, 2, 2, P], F32, name="tr")
             for q in range(2):
-                words = yraw[k][:, 2 * h + q, :].bitcast(F32)
+                words = yraw[h][:, q, :].bitcast(F32)
                 for u in range(2):
-                    nc.tensor.transpose(yb[k, h][:, q, u, :], words[:, u::2], ident[:])
+                    nc.tensor.transpose(yb[k, h][:, q, u, :], words[:, 256 * k + u : 256 * (k + 1) : 2], ident[:])
 
         def yc(k, h, eng="s"):
-            if h == 0:
+            if k not in yg:
                 yg[k] = new_group()
             copy(eng, yg[k][:, 2 * N * h : 2 * N * (h + 1)].bitcast(F32).rearrange("p (q r u) -> p q r u", q=2, u=2),
                  yb[k, h][:].rearrange("p q u r -> p q r u"))
@@ -256,232 +253,232 @@ def tile_split_tree_kinship_f5_kernel(tc, x_bytes, x_scale, wx, bx, lx, y, wy, b
             nc.sync.dma_start(out=ov[:, q, :], in_=dd[q][:])
 
         ctx.enter_context(tc.manual_schedule(engines={ENG.DVE, ENG.Activation, ENG.PE}))
-        il("x", 0, 0, "s")
-        il("x", 1, 0, "v")
+        il("x", 0, 0, "v")
+        il("x", 0, 1, "s")
         qw("x", 0, 0)
-        qw("x", 1, 0)
         xs(0)
         xs(1)
-        il("x", 0, 1, "s")
         xt(0)
-        xs(2)
-        xt(1)
-        xs(3)
-        xt(2)
         xc(0)
-        xc(1)
-        il("y", 0, 0, "v")
-        xt(3)
-        xc(2)
-        xc(3)
+        xt(1)
+        xs(2)
+        xt(2)
+        il("x", 1, 0, "s")
+        il("x", 1, 1, "v")
         qw("x", 0, 1)
-        il("y", 0, 1, "s")
-        xq(0, 0)
-        xq(0, 1)
-        qw("y", 0, 0)
-        ma(0, 0, 0)
+        qw("x", 1, 1)
+        il("y", 0, 0, "s")
+        qw("x", 1, 0)
+        xs(3)
         il("g", 0, 1, "v")
+        xt(3)
+        il("g", 0, 0, "s")
+        qw("y", 0, 0)
+        xs(4)
+        il("y", 0, 1, "s")
+        xs(5)
+        il("y", 1, 1, "v")
+        il("y", 1, 0, "s")
+        xs(6)
+        qw("y", 1, 1)
+        qw("g", 0, 0)
+        il("g", 1, 0, "s")
+        il("g", 1, 1, "v")
+        qw("g", 0, 1)
+        qw("g", 1, 1)
+        xc(1)
+        qw("g", 1, 0)
+        xc(2)
+        yt(0, 0)
+        qw("y", 1, 0)
+        xc(3)
+        yt(1, 0)
+        il("y", 2, 1, "v")
+        yc(0, 0)
+        yt(2, 0)
+        yc(1, 0)
+        yt(0, 1)
+        qw("y", 0, 1)
+        yc(2, 0)
+        yt(1, 1)
+        qw("y", 2, 1)
+        yc(0, 1)
+        yt(2, 1)
+        il("g", 2, 0, "v")
+        yc(1, 1)
+        xt(4)
+        yc(2, 1)
+        xt(5)
+        il("g", 2, 1, "s")
+        yq(0)
+        xt(6)
+        yq(1)
+        yq(2)
+        qw("g", 2, 0)
+        mb(1, 0, "y")
+        il("y", 2, 0, "s")
+        qw("g", 2, 1)
+        mb(1, 1, "y")
+        xs(7)
+        mb(1, 0, "g")
+        xq(0, 0)
+        mb(1, 1, "g")
+        xc(4)
+        qw("y", 2, 0)
+        xc(5)
+        mb(1, 2, "g")
+        xq(0, 1)
+        xc(6)
+        xs(8)
+        xt(7)
+        tb(1, 0, "g")
+        xs(9)
+        xc(7)
+        mb(1, 3, "g")
+        tb(1, 1, "g")
+        xt(8)
+        xq(1, 0)
+        tb(1, 2, "g")
+        mb(1, 2, "y")
+        xq(1, 1)
+        tb(1, 3, "g")
+        bts(1, 0)
+        mb(1, 3, "y")
+        tb(1, 0, "y")
+        bts(1, 1)
+        bts(1, 2)
+        tb(1, 1, "y")
+        ma(1, 1, 0)
+        bts(1, 3)
+        xs(10)
+        tb(1, 2, "y")
+        ma(1, 1, 1)
+        tb(1, 3, "y")
+        ma(1, 1, 2)
+        xs(11)
+        ta(1, 1, 0)
+        ma(1, 1, 3)
+        ta(1, 1, 1)
+        ma(1, 0, 0)
+        bm(1)
+        ta(1, 1, 2)
+        ma(1, 0, 1)
+        ma(1, 0, 2)
+        ta(1, 1, 3)
+        ma(1, 0, 3)
+        ta(1, 0, 0)
+        mb(0, 0, "g")
+        ta(1, 0, 1)
+        am(1, 1)
+        ta(1, 0, 2)
+        mb(0, 1, "g")
+        ta(1, 0, 3)
+        mb(0, 2, "g")
+        tb(0, 0, "g")
+        tb(0, 1, "g")
+        mb(0, 3, "g")
+        bq(1)
+        tb(0, 2, "g")
+        aq(1, 1)
+        ma(0, 0, 0)
+        tb(0, 3, "g")
+        am(1, 0)
         ma(0, 0, 1)
         ta(0, 0, 0)
         ma(0, 0, 2)
         ta(0, 0, 1)
         ma(0, 0, 3)
-        xs(4)
         ta(0, 0, 2)
-        ta(0, 0, 3)
-        xs(5)
-        xt(4)
-        il("g", 0, 0, "s")
-        am(0, 0)
-        xt(5)
-        xc(4)
-        xs(6)
-        xc(5)
-        yt(0, 0)
-        il("y", 1, 0, "s")
-        yt(0, 1)
-        aq(0, 0)
-        xt(6)
-        xs(7)
-        qw("g", 0, 0)
-        xc(6)
-        qw("y", 1, 0)
-        yc(0, 0)
-        xt(7)
-        il("g", 1, 0, "v")
-        yc(0, 1)
-        yt(1, 0)
-        xc(7)
-        yt(1, 1)
-        yq(0)
-        yc(1, 0)
-        yt(2, 0)
-        xq(1, 0)
-        yc(1, 1)
-        yt(2, 1)
-        xq(1, 1)
-        yc(2, 0)
-        il("y", 2, 0, "v")
-        ma(1, 0, 0)
-        yc(2, 1)
-        ma(1, 0, 1)
-        ta(1, 0, 0)
-        ma(1, 0, 2)
-        yq(1)
-        ta(1, 0, 1)
-        ma(1, 0, 3)
-        il("g", 2, 1, "v")
-        ta(1, 0, 2)
-        ta(1, 0, 3)
-        qw("y", 2, 0)
-        il("y", 2, 1, "s")
-        qw("g", 2, 1)
-        xs(8)
-        xs(9)
-        xt(8)
-        il("y", 1, 1, "s")
-        xs(10)
-        xt(9)
-        xs(11)
-        xt(10)
-        xc(8)
-        xc(9)
-        yq(2)
-        xt(11)
-        xc(10)
-        qw("y", 2, 1)
         mb(0, 0, "y")
-        il("g", 2, 0, "v")
-        xc(11)
+        bts(0, 0)
+        ta(0, 0, 3)
+        aq(1, 0)
         mb(0, 1, "y")
         tb(0, 0, "y")
+        am(0, 0)
         mb(0, 2, "y")
-        xq(2, 0)
+        xc(8)
         tb(0, 1, "y")
-        xq(2, 1)
-        il("g", 1, 1, "s")
         mb(0, 3, "y")
-        qw("g", 2, 0)
-        ma(2, 0, 0)
-        am(1, 0)
-        ma(2, 0, 1)
-        ma(2, 0, 2)
         tb(0, 2, "y")
-        tb(0, 3, "y")
-        ma(2, 0, 3)
-        qw("y", 1, 1)
-        ta(2, 0, 0)
-        aq(1, 0)
-        ta(2, 0, 1)
-        qw("g", 1, 0)
-        ta(2, 0, 2)
-        qw("y", 0, 1)
-        mb(0, 0, "g")
-        ta(2, 0, 3)
-        qw("g", 1, 1)
-        il("x", 1, 1, "s")
-        mb(0, 1, "g")
-        am(2, 0)
-        mb(0, 2, "g")
-        mb(0, 3, "g")
-        tb(0, 0, "g")
-        qw("g", 0, 1)
-        mb(1, 0, "y")
-        tb(0, 1, "g")
-        bts(0, 0)
-        mb(1, 0, "g")
-        aq(2, 0)
-        tb(0, 2, "g")
+        xt(9)
         bts(0, 1)
-        tb(0, 3, "g")
-        mb(1, 1, "g")
+        tb(0, 3, "y")
         bts(0, 2)
-        qw("x", 1, 1)
-        tb(1, 0, "g")
-        mb(1, 2, "g")
+        xt(10)
+        xc(9)
         bts(0, 3)
-        tb(1, 1, "g")
-        bts(1, 0)
+        aq(0, 0)
+        xt(11)
+        xc(10)
         bm(0)
-        ma(1, 1, 0)
-        tb(1, 2, "g")
-        ma(1, 1, 1)
-        ta(1, 1, 0)
-        ma(1, 1, 2)
-        ta(1, 1, 1)
-        ma(1, 1, 3)
-        ta(1, 1, 2)
-        bts(1, 1)
-        mb(1, 3, "g")
-        bq(0)
-        ta(1, 1, 3)
-        bts(1, 2)
-        tb(1, 0, "y")
-        mb(1, 1, "y")
-        am(1, 1)
-        tb(1, 3, "g")
-        mb(1, 2, "y")
-        tb(1, 1, "y")
-        mb(1, 3, "y")
-        tb(1, 2, "y")
-        bts(1, 3)
         ma(0, 1, 0)
-        tb(1, 3, "y")
-        aq(1, 1)
+        xc(11)
         ma(0, 1, 1)
         ta(0, 1, 0)
-        bm(1)
         ma(0, 1, 2)
         ta(0, 1, 1)
         ma(0, 1, 3)
         ta(0, 1, 2)
-        ma(2, 1, 0)
+        xq(2, 0)
         ta(0, 1, 3)
+        bq(0)
+        xq(2, 1)
+        mc(4)
+        am(0, 1)
+        ma(2, 0, 0)
+        ma(2, 0, 1)
+        ta(2, 0, 0)
+        ma(2, 0, 2)
+        ta(2, 0, 1)
+        ma(2, 0, 3)
+        ta(2, 0, 2)
+        st(4)
+        ma(2, 1, 0)
+        ta(2, 0, 3)
+        aq(0, 1)
         ma(2, 1, 1)
         ta(2, 1, 0)
-        am(0, 1)
-        ma(2, 1, 2)
+        am(2, 0)
+        mc(0)
         ta(2, 1, 1)
+        mc(1)
+        ex_(4)
+        mc(2)
+        ma(2, 1, 2)
+        st(0)
         ma(2, 1, 3)
         ta(2, 1, 2)
-        ta(2, 1, 3)
-        bq(1)
-        aq(0, 1)
-        mc(4)
-        am(2, 1)
-        mc(0)
-        mc(1)
-        st(0)
-        st(1)
-        mc(2)
-        ex_(0)
-        aq(2, 1)
+        aq(2, 0)
         mc(3)
-        ex_(1)
+        ex_(0)
+        st(1)
+        ta(2, 1, 3)
         st(2)
+        mc(5)
+        ex_(1)
         st(3)
-        mc(8)
+        mc(6)
         ex_(2)
-        st(4)
-        mc(9)
+        am(2, 1)
+        mc(7)
         ex_(3)
+        st(5)
+        aq(2, 1)
+        ex_(5)
+        st(6)
+        mc(8)
+        st(7)
+        mc(9)
+        ex_(6)
         st(8)
         mc(10)
-        ex_(4)
+        ex_(7)
         st(9)
         mc(11)
         ex_(8)
         st(10)
-        mc(5)
         ex_(9)
         st(11)
-        mc(6)
         ex_(10)
-        st(5)
-        mc(7)
         ex_(11)
-        st(6)
-        ex_(5)
-        st(7)
-        ex_(6)
-        ex_(7)

from contextlib import ExitStack

import concourse.mybir as mybir
from concourse.masks import make_identity

M, N, KX, KY, D = 1536, 512, 1024, 1536, 1024
RATE = 2.0
FLOPS = 2 * M * KX * D + 2 * 2 * N * KY * D + 2 * M * N * D

F32 = mybir.dt.float32
BF16 = mybir.dt.bfloat16
U32 = mybir.dt.uint32
U8 = mybir.dt.uint8
FP8 = mybir.dt.float8_e4m3fn
FP8X4 = mybir.dt.float8_e4m3fn_x4
ACT = mybir.ActivationFunctionType
ALU = mybir.AluOpType
ENG = mybir.EngineType

P = 128
PACK = 4
KP = P * PACK
GROUPS = D // KP
TOK = 512
NT = M // TOK
QT = TOK // P
XP = KX // KP
YP = KY // KP


def tile_split_tree_kinship_f5_kernel(tc, x_bytes, x_scale, wx, bx, lx, y, wy, by, wg, bg, ly, ex, ey, out):
    nc = tc.nc
    with ExitStack() as ctx:
        keep = ctx.enter_context(tc.tile_pool(name="keep", bufs=1))
        rawp = ctx.enter_context(tc.tile_pool(name="rawp", bufs=6))
        inx = ctx.enter_context(tc.tile_pool(name="inx", bufs=2))
        iny = ctx.enter_context(tc.tile_pool(name="iny", bufs=2))
        xsp = ctx.enter_context(tc.tile_pool(name="xsp", bufs=3))
        tnh = ctx.enter_context(tc.tile_pool(name="tnh", bufs=4))
        grp = ctx.enter_context(tc.tile_pool(name="grp", bufs=8))
        fin = ctx.enter_context(tc.tile_pool(name="fin", bufs=4))
        ps1 = ctx.enter_context(tc.psum_pool(name="ps1", bufs=5))
        ps2 = ctx.enter_context(tc.psum_pool(name="ps2", bufs=3))

        ident = keep.tile([P, P], F32, name="ident")
        make_identity(nc, ident[:])
        scale_b = keep.tile([P, KX], F32, name="scale_b", align_bytes=64)
        warm = keep.tile([P, 1], F32, name="warm")
        nc.vector.memset(warm[:], 0.0)
        nc.scalar.activation(out=warm[:], in_=warm[:], func=ACT.Tanh)

        raws, x8, yraw, vecs = {}, {}, {}, {}
        wsrc = {"x": wx, "y": wy, "g": wg}

        def load_w(nm, k):
            raws[nm, k] = rawp.tile([P, PACK, D], BF16, name="raw")
            nc.sync.dma_start(out=raws[nm, k][:], in_=wsrc[nm].rearrange("(k p j) c -> k p j c", p=P, j=PACK)[k])

        xv = x_bytes.rearrange("(p q) k -> p q k", q=M // P)
        yv = y.rearrange("(h q p) k -> h p q k", q=2, p=P)

        def load_x(i, lo=0, hi=QT):
            if lo == 0:
                x8[i] = inx.tile([P, QT, KX], U8, name="x8")
            nc.sync.dma_start(out=x8[i][:, lo:hi, :], in_=xv[:, QT * i + lo : QT * i + hi, :])

        def load_y(h):
            yraw[h] = iny.tile([P, 2, KY], BF16, name="yraw")
            nc.sync.dma_start(out=yraw[h][:], in_=yv[h])

        def load_scale():
            nc.sync.dma_start(out=scale_b[:], in_=x_scale.rearrange("o k -> (o k)").partition_broadcast(P))

        def load_vecs():
            for nm, v in (("bx", bx), ("lx", lx), ("by", by), ("bg", bg), ("ly", ly)):
                vecs[nm] = keep.tile([P, GROUPS, PACK], BF16, name="v_" + nm)
                nc.sync.dma_start(out=vecs[nm][:], in_=v.rearrange("(g p t) -> p g t", p=P, t=PACK))

        exb = keep.tile([P, M // P], BF16, name="exb")
        eyb = keep.tile([P, N], BF16, name="eyb")

        def load_e():
            nc.sync.dma_start(out=exb[:], in_=ex.rearrange("(p q) -> p q", q=M // P))
            nc.sync.dma_start(out=eyb[:], in_=ey.partition_broadcast(P))

        load_w("x", 0)
        load_scale()
        load_x(0)
        load_w("x", 1)
        load_w("y", 0)
        load_w("g", 0)
        load_x(1)
        load_w("y", 1)
        load_w("g", 1)
        load_y(0)
        load_y(1)
        load_w("y", 2)
        load_w("g", 2)
        load_x(2)
        load_vecs()
        load_e()

        bxf = keep.tile([P, GROUPS, PACK], F32, name="bxf")
        byf = keep.tile([P, GROUPS, PACK], F32, name="byf")
        bgh = keep.tile([P, GROUPS, PACK], F32, name="bgh")
        lyh = keep.tile([P, GROUPS, PACK], F32, name="lyh")
        lxf = keep.tile([P, GROUPS, PACK], F32, name="lxf")
        nex = keep.tile([P, M // P], F32, name="nex")
        nc.gpsimd.tensor_copy(out=bxf[:], in_=vecs["bx"][:])
        nc.gpsimd.tensor_copy(out=byf[:], in_=vecs["by"][:])
        nc.gpsimd.tensor_copy(out=lxf[:], in_=vecs["lx"][:])
        nc.gpsimd.tensor_scalar(out=bgh[:], in0=vecs["bg"][:], scalar1=0.5, scalar2=None, op0=ALU.mult)
        nc.gpsimd.tensor_scalar(out=lyh[:], in0=vecs["ly"][:], scalar1=0.5, scalar2=None, op0=ALU.mult)
        nc.gpsimd.tensor_scalar(out=nex[:], in0=exb[:], scalar1=-1.0, scalar2=None, op0=ALU.mult)

        def copy(eng, out, in_):
            if eng == "s":
                nc.scalar.copy(out=out, in_=in_)
            else:
                nc.vector.tensor_copy(out=out, in_=in_)

        def quant(key, src):
            code = keep.tile([P, KP], U32, name="code_" + key, align_bytes=64)
            sc = keep.tile([P, KP], U8, name="scal_" + key, align_bytes=64)
            nc.vector.quantize_mx(out=code[:].bitcast(FP8X4), scales=sc[:], in_=src)
            return code, sc

        def new_group():
            return grp.tile([P, PACK * KP], BF16, name="grouped", align_bytes=64)

        wc, wg_t = {}, {}

        def w_src(nm, k, c):
            return raws[nm, k][:, :, KP * c : KP * (c + 1)]

        def il(nm, k, c, eng):
            g = wg_t[nm, k, c] = new_group()
            copy(eng, g[:].rearrange("p (t m j) -> p m j t", t=PACK, j=PACK),
                 w_src(nm, k, c).rearrange("p j (m t) -> p m j t", t=PACK))

        def qw(nm, k, c):
            wc[nm, k, c] = quant("w%s%d%d" % (nm, k, c), wg_t[nm, k, c][:])

        xst, xb, xg, xc_ = {}, {}, {}, {}

        def xs(q):
            xst[q] = xsp.tile([P, KX], BF16, name="xs", align_bytes=64)
            nc.vector.tensor_tensor(out=xst[q][:], in0=x8[q // QT][:, q % QT, :].bitcast(FP8), in1=scale_b[:], op=ALU.mult)

        def xt(q):
            xb[q] = ps2.tile([P, XP, 2, P], F32, name="tr")
            words = xst[q][:].bitcast(F32)
            for k in range(XP):
                for u in range(2):
                    nc.tensor.transpose(xb[q][:, k, u, :], words[:, 256 * k + u : 256 * (k + 1) : 2], ident[:])

        def xc(q, eng="s"):
            i, r = divmod(q, QT)
            if (i, 0) not in xg:
                for k in range(XP):
                    xg[i, k] = new_group()
            for k in range(XP):
                copy(eng, xg[i, k][:, KP * r : KP * (r + 1)].bitcast(F32).rearrange("p (r u) -> p r u", u=2),
                     xb[q][:, k, :, :].rearrange("p u r -> p r u"))

        def xq(i, k):
            xc_[i, k] = quant("x%d%d" % (i, k), xg[i, k][:])

        yb, yg, yc_ = {}, {}, {}

        def yt(k, h):
            yb[k, h] = ps2.tile([P, 2, 2, P], F32, name="tr")
            for q in range(2):
                words = yraw[h][:, q, :].bitcast(F32)
                for u in range(2):
                    nc.tensor.transpose(yb[k, h][:, q, u, :], words[:, 256 * k + u : 256 * (k + 1) : 2], ident[:])

        def yc(k, h, eng="s"):
            if k not in yg:
                yg[k] = new_group()
            copy(eng, yg[k][:, 2 * N * h : 2 * N * (h + 1)].bitcast(F32).rearrange("p (q r u) -> p q r u", q=2, u=2),
                 yb[k, h][:].rearrange("p q u r -> p q r u"))

        def yq(k):
            yc_[k] = quant("y%d" % k, yg[k][:])

        def mx(bank, lhs, cols, rhs):
            for k in range(len(lhs)):
                (lc, ls), (rc, rs) = lhs[k], rhs[k]
                nc.tensor.matmul_mx(out=bank, lhsT=lc[:, cols].bitcast(FP8X4), lhsT_scale=ls[:, cols],
                                    rhs=rc[:].bitcast(FP8X4), rhs_scale=rs[:], start=(k == 0), stop=(k == len(lhs) - 1))

        def stepped(tile):
            return tile[:].rearrange("p t (c i) -> p c t i", i=4)

        def woven(tile):
            return tile[:].rearrange("p (c i t) -> p c t i", i=4, t=PACK)

        pb, tb_, pa, ta_, gb, ga, bc_, ac_, pc, dd = {}, {}, {}, {}, {}, {}, {}, {}, {}, {}

        def mb(c, t, nm):
            pb[c, t, nm] = ps1.tile([P, N], F32, name="s1")
            mx(pb[c, t, nm][:], [wc[nm, k, c] for k in range(YP)], slice(P * t, P * (t + 1)), [yc_[k] for k in range(YP)])

        def tb(c, t, nm):
            if (c, nm) not in tb_:
                tb_[c, nm] = tnh.tile([P, PACK, N], F32, name="tanh")
            b, s = (bgh, 0.5) if nm == "g" else (byf, 1.0)
            nc.scalar.activation(out=tb_[c, nm][:, t, :], in_=pb[c, t, nm][:], func=ACT.Tanh, bias=b[:, c, t : t + 1], scale=s)

        def bts(c, t):
            g = tb_[c, "g"][:, t, :]
            l = lyh[:, c, t : t + 1]
            nc.vector.tensor_scalar(out=g, in0=g, scalar1=l, scalar2=l, op0=ALU.mult, op1=ALU.add)

        def bm(c):
            gb[c] = new_group()
            nc.vector.tensor_tensor(out=woven(gb[c]), in0=stepped(tb_[c, "g"]), in1=stepped(tb_[c, "y"]), op=ALU.mult)

        def bq(c):
            bc_[c] = quant("b%d" % c, gb[c][:])

        def ma(i, c, t):
            pa[i, c, t] = ps1.tile([P, TOK], F32, name="s1")
            mx(pa[i, c, t][:], [wc["x", k, c] for k in range(XP)], slice(P * t, P * (t + 1)), [xc_[i, k] for k in range(XP)])

        def ta(i, c, t):
            if (i, c) not in ta_:
                ta_[i, c] = tnh.tile([P, PACK, TOK], F32, name="tanh")
            nc.scalar.activation(out=ta_[i, c][:, t, :], in_=pa[i, c, t][:], func=ACT.Tanh, bias=bxf[:, c, t : t + 1], scale=1.0)

        def am(i, c):
            ga[i, c] = new_group()
            l = lxf[:, c, :].unsqueeze(1).unsqueeze(3).to_broadcast([P, TOK // 4, PACK, 4])
            nc.vector.tensor_tensor(out=woven(ga[i, c]), in0=stepped(ta_[i, c]), in1=l, op=ALU.mult)

        def aq(i, c):
            ac_[i, c] = quant("a%d%d" % (i, c), ga[i, c][:])

        ov = out.rearrange("(p q) j -> p q j", q=M // P)

        def mc(q):
            i, r = divmod(q, QT)
            pc[q] = ps2.tile([P, N], F32, name="tr")
            mx(pc[q][:], [ac_[i, c] for c in range(GROUPS)], slice(P * r, P * (r + 1)), [bc_[c] for c in range(GROUPS)])

        def st(q):
            dd[q] = fin.tile([P, N], F32, name="d")
            nc.vector.scalar_tensor_tensor(out=dd[q][:], in0=pc[q][:], scalar=RATE / D**0.5, in1=eyb[:], op0=ALU.mult, op1=ALU.subtract)

        def ex_(q):
            nc.scalar.activation(out=dd[q][:], in_=dd[q][:], func=ACT.Exp, bias=nex[:, q : q + 1], scale=1.0)
            nc.sync.dma_start(out=ov[:, q, :], in_=dd[q][:])

        ctx.enter_context(tc.manual_schedule(engines={ENG.DVE, ENG.Activation, ENG.PE}))
        il("x", 0, 0, "v")
        il("x", 0, 1, "s")
        qw("x", 0, 0)
        xs(0)
        xs(1)
        xt(0)
        xc(0)
        xt(1)
        xs(2)
        xt(2)
        il("x", 1, 0, "s")
        il("x", 1, 1, "v")
        qw("x", 0, 1)
        qw("x", 1, 1)
        il("y", 0, 0, "s")
        qw("x", 1, 0)
        xs(3)
        il("g", 0, 1, "v")
        xt(3)
        il("g", 0, 0, "s")
        qw("y", 0, 0)
        xs(4)
        il("y", 0, 1, "s")
        xs(5)
        il("y", 1, 1, "v")
        il("y", 1, 0, "s")
        xs(6)
        qw("y", 1, 1)
        qw("g", 0, 0)
        il("g", 1, 0, "s")
        il("g", 1, 1, "v")
        qw("g", 0, 1)
        qw("g", 1, 1)
        xc(1)
        qw("g", 1, 0)
        xc(2)
        yt(0, 0)
        qw("y", 1, 0)
        xc(3)
        yt(1, 0)
        il("y", 2, 1, "v")
        yc(0, 0)
        yt(2, 0)
        yc(1, 0)
        yt(0, 1)
        qw("y", 0, 1)
        yc(2, 0)
        yt(1, 1)
        qw("y", 2, 1)
        yc(0, 1)
        yt(2, 1)
        il("g", 2, 0, "v")
        yc(1, 1)
        xt(4)
        yc(2, 1)
        xt(5)
        il("g", 2, 1, "s")
        yq(0)
        xt(6)
        yq(1)
        yq(2)
        qw("g", 2, 0)
        mb(1, 0, "y")
        il("y", 2, 0, "s")
        qw("g", 2, 1)
        mb(1, 1, "y")
        xs(7)
        mb(1, 0, "g")
        xq(0, 0)
        mb(1, 1, "g")
        xc(4)
        qw("y", 2, 0)
        xc(5)
        mb(1, 2, "g")
        xq(0, 1)
        xc(6)
        xs(8)
        xt(7)
        tb(1, 0, "g")
        xs(9)
        xc(7)
        mb(1, 3, "g")
        tb(1, 1, "g")
        xt(8)
        xq(1, 0)
        tb(1, 2, "g")
        mb(1, 2, "y")
        xq(1, 1)
        tb(1, 3, "g")
        bts(1, 0)
        mb(1, 3, "y")
        tb(1, 0, "y")
        bts(1, 1)
        bts(1, 2)
        tb(1, 1, "y")
        ma(1, 1, 0)
        bts(1, 3)
        xs(10)
        tb(1, 2, "y")
        ma(1, 1, 1)
        tb(1, 3, "y")
        ma(1, 1, 2)
        xs(11)
        ta(1, 1, 0)
        ma(1, 1, 3)
        ta(1, 1, 1)
        ma(1, 0, 0)
        bm(1)
        ta(1, 1, 2)
        ma(1, 0, 1)
        ma(1, 0, 2)
        ta(1, 1, 3)
        ma(1, 0, 3)
        ta(1, 0, 0)
        mb(0, 0, "g")
        ta(1, 0, 1)
        am(1, 1)
        ta(1, 0, 2)
        mb(0, 1, "g")
        ta(1, 0, 3)
        mb(0, 2, "g")
        tb(0, 0, "g")
        tb(0, 1, "g")
        mb(0, 3, "g")
        bq(1)
        tb(0, 2, "g")
        aq(1, 1)
        ma(0, 0, 0)
        tb(0, 3, "g")
        am(1, 0)
        ma(0, 0, 1)
        ta(0, 0, 0)
        ma(0, 0, 2)
        ta(0, 0, 1)
        ma(0, 0, 3)
        ta(0, 0, 2)
        mb(0, 0, "y")
        bts(0, 0)
        ta(0, 0, 3)
        aq(1, 0)
        mb(0, 1, "y")
        tb(0, 0, "y")
        am(0, 0)
        mb(0, 2, "y")
        xc(8)
        tb(0, 1, "y")
        mb(0, 3, "y")
        tb(0, 2, "y")
        xt(9)
        bts(0, 1)
        tb(0, 3, "y")
        bts(0, 2)
        xt(10)
        xc(9)
        bts(0, 3)
        aq(0, 0)
        xt(11)
        xc(10)
        bm(0)
        ma(0, 1, 0)
        xc(11)
        ma(0, 1, 1)
        ta(0, 1, 0)
        ma(0, 1, 2)
        ta(0, 1, 1)
        ma(0, 1, 3)
        ta(0, 1, 2)
        xq(2, 0)
        ta(0, 1, 3)
        bq(0)
        xq(2, 1)
        mc(4)
        am(0, 1)
        ma(2, 0, 0)
        ma(2, 0, 1)
        ta(2, 0, 0)
        ma(2, 0, 2)
        ta(2, 0, 1)
        ma(2, 0, 3)
        ta(2, 0, 2)
        st(4)
        ma(2, 1, 0)
        ta(2, 0, 3)
        aq(0, 1)
        ma(2, 1, 1)
        ta(2, 1, 0)
        am(2, 0)
        mc(0)
        ta(2, 1, 1)
        mc(1)
        ex_(4)
        mc(2)
        ma(2, 1, 2)
        st(0)
        ma(2, 1, 3)
        ta(2, 1, 2)
        aq(2, 0)
        mc(3)
        ex_(0)
        st(1)
        ta(2, 1, 3)
        st(2)
        mc(5)
        ex_(1)
        st(3)
        mc(6)
        ex_(2)
        am(2, 1)
        mc(7)
        ex_(3)
        st(5)
        aq(2, 1)
        ex_(5)
        st(6)
        mc(8)
        st(7)
        mc(9)
        ex_(6)
        st(8)
        mc(10)
        ex_(7)
        st(9)
        mc(11)
        ex_(8)
        st(10)
        ex_(9)
        st(11)
        ex_(10)
        ex_(11)
